import numpy as np
import ml_dtypes


def mxq(x, axis, fmt="e4m3"):
    dtype, down = {"e4m3": (ml_dtypes.float8_e4m3fn, 7), "e5m2": (ml_dtypes.float8_e5m2, 14)}[fmt]
    v = np.moveaxis(np.asarray(x, np.float32).astype(ml_dtypes.bfloat16).astype(np.float64), axis, -1)
    blocks = v.reshape(v.shape[:-1] + (-1, 32))
    amax = np.abs(blocks).max(-1, keepdims=True)
    byte = np.maximum(np.where(amax > 0, np.frexp(amax)[1] - 1 + 127, 0) - down, 1)
    scale = np.exp2(byte - 127.0)
    codes = (blocks / scale).astype(np.float32).astype(dtype).astype(np.float64)
    return np.moveaxis((codes * scale).reshape(v.shape), -1, axis)


WIDE = False


def mx_kscale(k):
    if not WIDE:
        return np.ones(k)
    levels = np.array([24, -24, 12, -12, 0])
    if k % 512:
        return np.exp2(np.random.permutation(np.resize(levels, k // 32))).repeat(32)
    a = np.empty((k // 512, 16))
    for p in range(k // 512):
        a[p, :8] = np.random.permutation(np.resize(levels, 8))
        for g in range(8):
            far = levels[np.abs(levels - a[p, g]) >= 10]
            a[p, g + 8] = far[np.random.randint(len(far))]
    return np.exp2(a.ravel()).repeat(32)


def f64(x):
    return np.asarray(x).astype(np.float64)


def striped8(idx):
    return np.concatenate([v.reshape(-1, 16).T for v in idx]).astype(np.uint16)


def unstriped8(offs):
    return np.stack([offs[16 * g:16 * g + 16].T.reshape(-1) for g in range(8)]).astype(np.int64)


E2M1 = np.array([0.0, 0.5, 1.0, 1.5, 2.0, 3.0, 4.0, 6.0, -0.0, -0.5, -1.0, -1.5, -2.0, -3.0, -4.0, -6.0])


def pack_weight(w, fmt):
    k, n = w.shape
    w = f64(np.asarray(w, np.float32).astype(ml_dtypes.bfloat16)).reshape(k // 32, 32, n)
    amax = np.abs(w).max(1)
    if fmt == "e4m3":
        byte = np.frexp(amax)[1] - 1 + 127 - 7
    else:
        mant, ex = np.frexp(amax / 6.0)
        byte = np.where(mant > 0.5, ex, ex - 1) + 127
    byte = np.clip(np.where(amax > 0, byte, 1), 1, 254)
    scaled = (w * np.exp2(127.0 - byte)[:, None, :]).reshape(k, n).astype(np.float32)
    by_word = np.ascontiguousarray(scaled.reshape(k // 512, 128, 4, n).transpose(0, 1, 3, 2))
    if fmt == "e4m3":
        words = by_word.astype(ml_dtypes.float8_e4m3fn).view(np.uint8)
    else:
        c = by_word.astype(ml_dtypes.float4_e2m1fn).view(np.uint8) & 0xF
        words = (c[..., 0::2] | (c[..., 1::2] << 4)).reshape(k // 512, 128, 2 * n)
    return np.ascontiguousarray(words), np.ascontiguousarray(byte.astype(np.uint8).reshape(k // 512, 16, n))


def unpack_weight(words, scales, fmt):
    g, _, n = scales.shape
    words = np.ascontiguousarray(words).reshape(g, 128, n, -1)
    if fmt == "e4m3":
        vals = words.view(ml_dtypes.float8_e4m3fn).astype(np.float64)
    else:
        nib = np.empty((g, 128, n, 4), np.uint8)
        nib[..., 0::2] = words & 0xF
        nib[..., 1::2] = words >> 4
        vals = E2M1[nib]
    vals = vals * np.repeat(np.exp2(scales.astype(np.float64) - 127.0), 8, axis=1)[..., None]
    return vals.transpose(0, 1, 3, 2).reshape(g * 512, n)


def planes(y):
    n, m = y.shape
    v = y.astype(np.float32).astype(ml_dtypes.bfloat16).astype(np.float64).reshape(n // 32, 32, m)
    top = np.abs(v).max(1)
    byte = np.clip(np.where(top > 0, np.frexp(top)[1] - 1 + 127 - 7, 1), 1, 254)
    codes = (v * np.exp2(127.0 - byte)[:, None, :]).reshape(n, m).astype(np.float32).astype(ml_dtypes.float8_e4m3fn).view(np.uint8)
    words = codes.reshape(n // 512, 128, 4, m).transpose(0, 1, 3, 2)
    return np.ascontiguousarray(words), np.ascontiguousarray(byte.astype(np.uint8).reshape(n // 512, 16, m))


def sigm(f):
    return 1.0 / (1.0 + np.exp(-np.maximum(f, -700.0)))


K, N, T, J = 1024, 512, 2048, 1024


def setup_inputs():
    n = np.random.standard_normal
    s = mx_kscale(K)[:, None]
    p_wk = pack_weight(n((K, N)) / np.sqrt(K) / s, "e2m1")
    p_wv = pack_weight(n((K, N)) / np.sqrt(K) / s, "e2m1")
    return {
        "xT": (n((K, T)) * s).astype(np.float32),
        "wgt": np.repeat(np.random.uniform(0.5, 2.0, (8, J)), 16, axis=0).astype(np.float32),
        "wk_words": p_wk[0],
        "wk_scales": p_wk[1],
        "wv_words": p_wv[0],
        "wv_scales": p_wv[1],
        "st": (n((N, J))).astype(np.float32),
        "offs": striped8(np.stack([np.random.permutation(T)[:J] for _ in range(8)])),
    }


def reference(xT, wgt, wk_words, wk_scales, wv_words, wv_scales, st, offs):
    idx = unstriped8(offs)
    rows = np.arange(K)
    xg = f64(wgt)[rows // 4 % 128] * f64(xT)[rows[:, None], idx[rows % 512 // 64]]
    xT_ = mxq(xg, 0, "e4m3")
    wk_ = unpack_weight(wk_words, wk_scales, "e2m1")
    wv_ = unpack_weight(wv_words, wv_scales, "e2m1")
    ke = wk_.T @ xT_
    ve = wv_.T @ xT_
    gate = sigm(ke * f64(st))
    out_0 = gate * ve
    return (out_0,) + planes(out_0)

@@ -1,0 +1,216 @@
+from contextlib import ExitStack
+
+import concourse.mybir as mybir
+
+K, N, T, J = 1024, 512, 2048, 1024
+FLOPS = 2 * 2 * K * N * J
+
+F32 = mybir.dt.float32
+BF16 = mybir.dt.bfloat16
+I32 = mybir.dt.int32
+U32 = mybir.dt.uint32
+U16 = mybir.dt.uint16
+U8 = mybir.dt.uint8
+FP8X4 = mybir.dt.float8_e4m3fn_x4
+FP4X4 = mybir.dt.float4_e2m1fn_x4
+MULT = mybir.AluOpType.mult
+SIGMOID = mybir.ActivationFunctionType.Sigmoid
+
+P = 128
+PACK = 4
+PASSES = 2
+H = 512
+
+
+def tile_list_sigP_kernel(tc, xT, wgt, wk_words, wk_scales, wv_words, wv_scales, st, offs, out_0, out_1, out_2):
+    nc = tc.nc
+    with ExitStack() as ctx:
+        sb = ctx.enter_context(tc.tile_pool(name="sb", bufs=1))
+        psum = ctx.enter_context(tc.psum_pool(name="psum", bufs=1))
+
+        def tile(shape, dtype, name):
+            return sb.tile(shape, dtype, name=name, align_bytes=64)
+
+        lists = sb.tile([P, J // 16], U16, name="lists")
+        nc.sync.dma_start(lists[:], offs)
+
+        raw_words, raw_scales = [], []
+        for w, words in enumerate((wk_words, wv_words)):
+            raw = tile([P, PASSES, 2 * N], U8, "raw_words%d" % w)
+            nc.sync.dma_start(out=raw[:].bitcast(I32), in_=words.rearrange("a p b -> p a b").bitcast(I32))
+            raw_words.append(raw)
+        for w, scales in enumerate((wk_scales, wv_scales)):
+            raw = tile([P, PASSES, N], U8, "raw_scales%d" % w)
+            nc.vector.memset(raw[:].bitcast(I32), 0)
+            raw_scales.append(raw)
+        for w, scales in enumerate((wk_scales, wv_scales)):
+            for q in range(4):
+                nc.scalar.dma_start(
+                    out=raw_scales[w][32 * q : 32 * q + 4, :, :].bitcast(I32),
+                    in_=scales[:, 4 * q : 4 * q + 4, :].rearrange("a r n -> r a n").bitcast(I32),
+                )
+
+        warm_in = tile([P, 1], F32, "warm_in")
+        warm_out = tile([P, 1], F32, "warm_out")
+        nc.vector.memset(warm_in[:], 0.0)
+        nc.scalar.activation(out=warm_out[:], in_=warm_in[:], func=SIGMOID)
+
+        late = tile([P, PACK * H], F32, "late")
+        wgt_h = [late[:, 2 * H : 3 * H], tile([P, H], F32, "wgt1")[:]]
+        x_planes = xT.rearrange("(a p i) t -> a i p t", a=PASSES, i=PACK)
+        x = [tile([P, T], F32, "x%d" % g) for g in range(PASSES * PACK)]
+        nc.sync.dma_start(out=wgt_h[0], in_=wgt[:, 0:H])
+        nc.sync.dma_start(out=x[0][:], in_=x_planes[0, 0])
+        nc.sync.dma_start(out=wgt_h[1], in_=wgt[:, H:J])
+        for g in range(1, PASSES * PACK):
+            nc.sync.dma_start(out=x[g][:], in_=x_planes[g // PACK, g % PACK])
+        st_rows = st.rearrange("(p t) j -> p t j", t=PACK)
+        st_h = []
+        for h in range(2):
+            s = tile([P, PACK, H], F32, "st%d" % h)
+            nc.sync.dma_start(out=s[:], in_=st_rows[:, :, h * H : (h + 1) * H])
+            st_h.append(s)
+
+        w_words = [tile([P, PASSES, PACK, 2 * P], U8, "w_words%d" % w) for w in range(2)]
+        w_scales = [tile([P, PASSES, PACK, P], U8, "w_scales%d" % w) for w in range(2)]
+        for w in range(2):
+            nc.vector.tensor_copy(
+                out=w_words[w][:].bitcast(U16),
+                in_=raw_words[w][:].bitcast(U16).rearrange("p a (q t) -> p a t q", t=PACK),
+            )
+
+        def deal_scales(w):
+            nc.vector.tensor_copy(out=w_scales[w][:], in_=raw_scales[w][:].rearrange("p a (q t) -> p a t q", t=PACK))
+
+        picked = {}
+        for a, h in ((0, 0), (0, 1), (1, 0)):
+            picked[(a, h)] = tile([P, PACK * H], F32, "picked%d%d" % (a, h))[:]
+        picked[(1, 1)] = late[:, 0 : PACK * H]
+        woven = {}
+        for a in range(PASSES):
+            for h in range(2):
+                woven[(a, h)] = tile([P, PACK * H], BF16, "woven%d%d" % (a, h))[:]
+        x_codes, x_scales = {}, {}
+
+        def gather(g, h, c0=0, c1=H):
+            a, i = divmod(g, PACK)
+            nc.vector.tensor_tensor(
+                picked[(a, h)][:, i * H + c0 : i * H + c1],
+                x[g][:].indirect(lists[:, (h * H + c0) // 16 : (h * H + c1) // 16]),
+                wgt_h[h][:, c0:c1],
+                MULT,
+            )
+
+        def weave(copy, dst, src):
+            copy(out=dst.rearrange("p (c i t) -> p c t i", i=4, t=PACK), in_=src.rearrange("p t (c i) -> p c t i", i=4))
+
+        def weave_x(a, h, c0=0, c1=H):
+            planes = picked[(a, h)].rearrange("p (t j) -> p t j", t=PACK)
+            weave(nc.scalar.copy, woven[(a, h)][:, PACK * c0 : PACK * c1], planes[:, :, c0:c1])
+
+        def quantise_x(a, h):
+            x_codes[(a, h)] = tile([P, H], U32, "woven10" if (a, h) == (0, 1) else "x_codes%d%d" % (a, h))
+            x_scales[(a, h)] = tile([P, H], U8, "x_scales%d%d" % (a, h))
+            nc.vector.quantize_mx(out=x_codes[(a, h)][:].bitcast(FP8X4), scales=x_scales[(a, h)][:], in_=woven[(a, h)])
+
+        banks = {}
+
+        def product(w, t, a, h):
+            if a == 0:
+                banks[(w, t, h)] = psum.tile([P, H], F32, name="bank%d%d" % (w, t))
+            nc.tensor.matmul_mx(
+                out=banks[(w, t, h)][:],
+                lhsT=w_words[w][:, a, t, :].bitcast(FP4X4),
+                lhsT_scale=w_scales[w][:, a, t, :],
+                rhs=x_codes[(a, h)][:].bitcast(FP8X4),
+                rhs_scale=x_scales[(a, h)][:],
+                start=(a == 0),
+                stop=(a == PASSES - 1),
+            )
+
+        C = H // 2
+        deal_scales(0)
+        deal_scales(1)
+        for g in range(4):
+            gather(g, 0)
+            gather(g, 1)
+        weave_x(0, 0)
+        weave_x(0, 1)
+        gather(4, 0)
+        gather(4, 1)
+        quantise_x(0, 0)
+        for w in range(2):
+            for t in range(PACK):
+                product(w, t, 0, 0)
+        gather(5, 0)
+        gather(5, 1)
+        gather(6, 0)
+        for c in range(2):
+            gather(7, 0, c * C, (c + 1) * C)
+            weave_x(1, 0, c * C, (c + 1) * C)
+        gather(6, 1)
+        for c in range(2):
+            gather(7, 1, c * C, (c + 1) * C)
+            weave_x(1, 1, c * C, (c + 1) * C)
+        quantise_x(1, 0)
+        quantise_x(0, 1)
+        for w in range(2):
+            for t in range(PACK):
+                product(w, t, 1, 0)
+
+        gates = {}
+        y = [tile([P, PACK, H], F32, "y%d" % h) for h in range(2)]
+        y_rows = out_0.rearrange("(p t) j -> p t j", t=PACK)
+        y_codes = tile([P, J], U32, "y_codes")
+        y_scales = tile([P, J], U8, "y_scales")
+        words_out = out_1[0].rearrange("p j i -> p (j i)").bitcast(I32)
+
+        def gate(t, h):
+            logit = tile([P, H], F32, "logit%d" % t)
+            nc.vector.tensor_tensor(logit[:], banks[(0, t, h)][:], st_h[h][:, t, :], MULT)
+            gates[(t, h)] = tile([P, H], F32, "gate%d%d" % (t, h))
+            nc.scalar.activation(out=gates[(t, h)][:], in_=logit[:], func=SIGMOID)
+
+        def let_through(t, h, c0, c1):
+            nc.vector.tensor_tensor(y[h][:, t, c0:c1], banks[(1, t, h)][:, c0:c1], gates[(t, h)][:, c0:c1], MULT)
+
+        def store_y(h, t0, t1, c0, c1):
+            nc.sync.dma_start(out=y_rows[:, t0:t1, h * H + c0 : h * H + c1], in_=y[h][:, t0:t1, c0:c1])
+
+        def quantise_y(src, j0, j1):
+            nc.vector.quantize_mx(out=y_codes[:, j0:j1].bitcast(FP8X4), scales=y_scales[:, j0:j1], in_=src)
+            nc.sync.dma_start(out=words_out[:, j0:j1], in_=y_codes[:, j0:j1].bitcast(I32))
+
+        for t in range(PACK):
+            gate(t, 0)
+            if t == 1:
+                quantise_x(1, 1)
+        for t in range(PACK):
+            product(0, t, 0, 1)
+            product(0, t, 1, 1)
+        for t in range(PACK):
+            let_through(t, 0, 0, H)
+            store_y(0, t, t + 1, 0, H)
+            product(1, t, 0, 1)
+            product(1, t, 1, 1)
+        yb0 = tile([P, PACK * H], BF16, "yb0")
+        for t in range(PACK):
+            gate(t, 1)
+        for c in range(2):
+            weave(nc.scalar.copy, yb0[:, c * PACK * C : (c + 1) * PACK * C], y[0][:, :, c * C : (c + 1) * C])
+        yb1 = [tile([P, PACK * C], BF16, "yb1%d" % c) for c in range(2)]
+        for t in range(PACK):
+            let_through(t, 1, 0, C)
+        store_y(1, 0, PACK, 0, C)
+        weave(nc.scalar.copy, yb1[0][:], y[1][:, :, 0:C])
+        for t in range(PACK):
+            let_through(t, 1, C, H)
+            if t % 2 == 1:
+                store_y(1, t - 1, t + 1, C, H)
+        quantise_y(yb0[:], 0, H)
+        weave(nc.vector.tensor_copy, yb1[1][:], y[1][:, :, C:H])
+        quantise_y(yb1[0][:], H, H + C)
+        quantise_y(yb1[1][:], H + C, J)
+        for q in range(4):
+            queue = nc.scalar if q % 2 else nc.sync
+            queue.dma_start(out=out_2[0, 4 * q : 4 * q + 4, :].bitcast(I32), in_=y_scales[32 * q : 32 * q + 4, :].bitcast(I32))

@@ -14,6 +14,7 @@ U8 = mybir.dt.uint8
 FP8X4 = mybir.dt.float8_e4m3fn_x4
 FP4X4 = mybir.dt.float4_e2m1fn_x4
 MULT = mybir.AluOpType.mult
+ADD = mybir.AluOpType.add
 SIGMOID = mybir.ActivationFunctionType.Sigmoid
 
 P = 128
@@ -154,9 +155,8 @@ def tile_list_sigP_kernel(tc, xT, wgt, wk_words, wk_scales, wv_words, wv_scales,
             weave_x(1, 1, c * C, (c + 1) * C)
         quantise_x(1, 0)
         quantise_x(0, 1)
-        for w in range(2):
-            for t in range(PACK):
-                product(w, t, 1, 0)
+        for w, t in ((0, 0), (0, 1), (1, 0), (0, 2), (1, 1), (0, 3), (1, 2), (1, 3)):
+            product(w, t, 1, 0)
 
         gates = {}
         y = [tile([P, PACK, H], F32, "y%d" % h) for h in range(2)]
@@ -181,23 +181,42 @@ def tile_list_sigP_kernel(tc, xT, wgt, wk_words, wk_scales, wv_words, wv_scales,
             nc.vector.quantize_mx(out=y_codes[:, j0:j1].bitcast(FP8X4), scales=y_scales[:, j0:j1], in_=src)
             nc.sync.dma_start(out=words_out[:, j0:j1], in_=y_codes[:, j0:j1].bitcast(I32))
 
+        def let_through_on_gpsimd(t):
+            values = tile([P, H], F32, "woven11" if t == 0 else "values%d" % t)
+            nc.scalar.copy(out=values[:], in_=banks[(1, t, 0)][:])
+            nc.gpsimd.tensor_tensor(y[0][:, t, :], values[:], gates[(t, 0)][:], MULT)
+
+        def second_half(w, t):
+            for a in range(PASSES):
+                product(w, t, a, 1)
+
         for t in range(PACK):
             gate(t, 0)
-            if t == 1:
+            if t == 0:
                 quantise_x(1, 1)
-        for t in range(PACK):
-            product(0, t, 0, 1)
-            product(0, t, 1, 1)
-        for t in range(PACK):
+            second_half(0, t)
+            if t < 2:
+                let_through_on_gpsimd(t)
+                store_y(0, t, t + 1, 0, H)
+                second_half(1, t)
+        for t in range(2):
+            gate(t, 1)
+        for t in range(2, PACK):
             let_through(t, 0, 0, H)
             store_y(0, t, t + 1, 0, H)
-            product(1, t, 0, 1)
-            product(1, t, 1, 1)
-        yb0 = tile([P, PACK * H], BF16, "yb0")
-        for t in range(PACK):
+            second_half(1, t)
+        for t in range(2, PACK):
             gate(t, 1)
+        yb0 = tile([P, PACK * H], BF16, "yb0")
         for c in range(2):
-            weave(nc.scalar.copy, yb0[:, c * PACK * C : (c + 1) * PACK * C], y[0][:, :, c * C : (c + 1) * C])
+            nc.gpsimd.tensor_scalar(
+                yb0[:, c * PACK * C : (c + 1) * PACK * C].rearrange("p (j t) -> p j t", t=PACK),
+                y[0][:, :, c * C : (c + 1) * C].rearrange("p t j -> p j t"),
+                1.0,
+                -0.0,
+                MULT,
+                ADD,
+            )
         yb1 = [tile([P, PACK * C], BF16, "yb1%d" % c) for c in range(2)]
         for t in range(PACK):
             let_through(t, 1, 0, C)

from contextlib import ExitStack

import concourse.mybir as mybir

K, N, T, J = 1024, 512, 2048, 1024
FLOPS = 2 * 2 * K * N * J

F32 = mybir.dt.float32
BF16 = mybir.dt.bfloat16
I32 = mybir.dt.int32
U32 = mybir.dt.uint32
U16 = mybir.dt.uint16
U8 = mybir.dt.uint8
FP8X4 = mybir.dt.float8_e4m3fn_x4
FP4X4 = mybir.dt.float4_e2m1fn_x4
MULT = mybir.AluOpType.mult
ADD = mybir.AluOpType.add
SIGMOID = mybir.ActivationFunctionType.Sigmoid

P = 128
PACK = 4
PASSES = 2
H = 512


def tile_list_sigP_kernel(tc, xT, wgt, wk_words, wk_scales, wv_words, wv_scales, st, offs, out_0, out_1, out_2):
    nc = tc.nc
    with ExitStack() as ctx:
        sb = ctx.enter_context(tc.tile_pool(name="sb", bufs=1))
        psum = ctx.enter_context(tc.psum_pool(name="psum", bufs=1))

        def tile(shape, dtype, name):
            return sb.tile(shape, dtype, name=name, align_bytes=64)

        lists = sb.tile([P, J // 16], U16, name="lists")
        nc.sync.dma_start(lists[:], offs)

        raw_words, raw_scales = [], []
        for w, words in enumerate((wk_words, wv_words)):
            raw = tile([P, PASSES, 2 * N], U8, "raw_words%d" % w)
            nc.sync.dma_start(out=raw[:].bitcast(I32), in_=words.rearrange("a p b -> p a b").bitcast(I32))
            raw_words.append(raw)
        for w, scales in enumerate((wk_scales, wv_scales)):
            raw = tile([P, PASSES, N], U8, "raw_scales%d" % w)
            nc.vector.memset(raw[:].bitcast(I32), 0)
            raw_scales.append(raw)
        for w, scales in enumerate((wk_scales, wv_scales)):
            for q in range(4):
                nc.scalar.dma_start(
                    out=raw_scales[w][32 * q : 32 * q + 4, :, :].bitcast(I32),
                    in_=scales[:, 4 * q : 4 * q + 4, :].rearrange("a r n -> r a n").bitcast(I32),
                )

        warm_in = tile([P, 1], F32, "warm_in")
        warm_out = tile([P, 1], F32, "warm_out")
        nc.vector.memset(warm_in[:], 0.0)
        nc.scalar.activation(out=warm_out[:], in_=warm_in[:], func=SIGMOID)

        late = tile([P, PACK * H], F32, "late")
        wgt_h = [late[:, 2 * H : 3 * H], tile([P, H], F32, "wgt1")[:]]
        x_planes = xT.rearrange("(a p i) t -> a i p t", a=PASSES, i=PACK)
        x = [tile([P, T], F32, "x%d" % g) for g in range(PASSES * PACK)]
        nc.sync.dma_start(out=wgt_h[0], in_=wgt[:, 0:H])
        nc.sync.dma_start(out=x[0][:], in_=x_planes[0, 0])
        nc.sync.dma_start(out=wgt_h[1], in_=wgt[:, H:J])
        for g in range(1, PASSES * PACK):
            nc.sync.dma_start(out=x[g][:], in_=x_planes[g // PACK, g % PACK])
        st_rows = st.rearrange("(p t) j -> p t j", t=PACK)
        st_h = []
        for h in range(2):
            s = tile([P, PACK, H], F32, "st%d" % h)
            nc.sync.dma_start(out=s[:], in_=st_rows[:, :, h * H : (h + 1) * H])
            st_h.append(s)

        w_words = [tile([P, PASSES, PACK, 2 * P], U8, "w_words%d" % w) for w in range(2)]
        w_scales = [tile([P, PASSES, PACK, P], U8, "w_scales%d" % w) for w in range(2)]
        for w in range(2):
            nc.vector.tensor_copy(
                out=w_words[w][:].bitcast(U16),
                in_=raw_words[w][:].bitcast(U16).rearrange("p a (q t) -> p a t q", t=PACK),
            )

        def deal_scales(w):
            nc.vector.tensor_copy(out=w_scales[w][:], in_=raw_scales[w][:].rearrange("p a (q t) -> p a t q", t=PACK))

        picked = {}
        for a, h in ((0, 0), (0, 1), (1, 0)):
            picked[(a, h)] = tile([P, PACK * H], F32, "picked%d%d" % (a, h))[:]
        picked[(1, 1)] = late[:, 0 : PACK * H]
        woven = {}
        for a in range(PASSES):
            for h in range(2):
                woven[(a, h)] = tile([P, PACK * H], BF16, "woven%d%d" % (a, h))[:]
        x_codes, x_scales = {}, {}

        def gather(g, h, c0=0, c1=H):
            a, i = divmod(g, PACK)
            nc.vector.tensor_tensor(
                picked[(a, h)][:, i * H + c0 : i * H + c1],
                x[g][:].indirect(lists[:, (h * H + c0) // 16 : (h * H + c1) // 16]),
                wgt_h[h][:, c0:c1],
                MULT,
            )

        def weave(copy, dst, src):
            copy(out=dst.rearrange("p (c i t) -> p c t i", i=4, t=PACK), in_=src.rearrange("p t (c i) -> p c t i", i=4))

        def weave_x(a, h, c0=0, c1=H):
            planes = picked[(a, h)].rearrange("p (t j) -> p t j", t=PACK)
            weave(nc.scalar.copy, woven[(a, h)][:, PACK * c0 : PACK * c1], planes[:, :, c0:c1])

        def quantise_x(a, h):
            x_codes[(a, h)] = tile([P, H], U32, "woven10" if (a, h) == (0, 1) else "x_codes%d%d" % (a, h))
            x_scales[(a, h)] = tile([P, H], U8, "x_scales%d%d" % (a, h))
            nc.vector.quantize_mx(out=x_codes[(a, h)][:].bitcast(FP8X4), scales=x_scales[(a, h)][:], in_=woven[(a, h)])

        banks = {}

        def product(w, t, a, h):
            if a == 0:
                banks[(w, t, h)] = psum.tile([P, H], F32, name="bank%d%d" % (w, t))
            nc.tensor.matmul_mx(
                out=banks[(w, t, h)][:],
                lhsT=w_words[w][:, a, t, :].bitcast(FP4X4),
                lhsT_scale=w_scales[w][:, a, t, :],
                rhs=x_codes[(a, h)][:].bitcast(FP8X4),
                rhs_scale=x_scales[(a, h)][:],
                start=(a == 0),
                stop=(a == PASSES - 1),
            )

        C = H // 2
        deal_scales(0)
        deal_scales(1)
        for g in range(4):
            gather(g, 0)
            gather(g, 1)
        weave_x(0, 0)
        weave_x(0, 1)
        gather(4, 0)
        gather(4, 1)
        quantise_x(0, 0)
        for w in range(2):
            for t in range(PACK):
                product(w, t, 0, 0)
        gather(5, 0)
        gather(5, 1)
        gather(6, 0)
        for c in range(2):
            gather(7, 0, c * C, (c + 1) * C)
            weave_x(1, 0, c * C, (c + 1) * C)
        gather(6, 1)
        for c in range(2):
            gather(7, 1, c * C, (c + 1) * C)
            weave_x(1, 1, c * C, (c + 1) * C)
        quantise_x(1, 0)
        quantise_x(0, 1)
        for w, t in ((0, 0), (0, 1), (1, 0), (0, 2), (1, 1), (0, 3), (1, 2), (1, 3)):
            product(w, t, 1, 0)

        gates = {}
        y = [tile([P, PACK, H], F32, "y%d" % h) for h in range(2)]
        y_rows = out_0.rearrange("(p t) j -> p t j", t=PACK)
        y_codes = tile([P, J], U32, "y_codes")
        y_scales = tile([P, J], U8, "y_scales")
        words_out = out_1[0].rearrange("p j i -> p (j i)").bitcast(I32)

        def gate(t, h):
            logit = tile([P, H], F32, "logit%d" % t)
            nc.vector.tensor_tensor(logit[:], banks[(0, t, h)][:], st_h[h][:, t, :], MULT)
            gates[(t, h)] = tile([P, H], F32, "gate%d%d" % (t, h))
            nc.scalar.activation(out=gates[(t, h)][:], in_=logit[:], func=SIGMOID)

        def let_through(t, h, c0, c1):
            nc.vector.tensor_tensor(y[h][:, t, c0:c1], banks[(1, t, h)][:, c0:c1], gates[(t, h)][:, c0:c1], MULT)

        def store_y(h, t0, t1, c0, c1):
            nc.sync.dma_start(out=y_rows[:, t0:t1, h * H + c0 : h * H + c1], in_=y[h][:, t0:t1, c0:c1])

        def quantise_y(src, j0, j1):
            nc.vector.quantize_mx(out=y_codes[:, j0:j1].bitcast(FP8X4), scales=y_scales[:, j0:j1], in_=src)
            nc.sync.dma_start(out=words_out[:, j0:j1], in_=y_codes[:, j0:j1].bitcast(I32))

        def let_through_on_gpsimd(t):
            values = tile([P, H], F32, "woven11" if t == 0 else "values%d" % t)
            nc.scalar.copy(out=values[:], in_=banks[(1, t, 0)][:])
            nc.gpsimd.tensor_tensor(y[0][:, t, :], values[:], gates[(t, 0)][:], MULT)

        def second_half(w, t):
            for a in range(PASSES):
                product(w, t, a, 1)

        for t in range(PACK):
            gate(t, 0)
            if t == 0:
                quantise_x(1, 1)
            second_half(0, t)
            if t < 2:
                let_through_on_gpsimd(t)
                store_y(0, t, t + 1, 0, H)
                second_half(1, t)
        for t in range(2):
            gate(t, 1)
        for t in range(2, PACK):
            let_through(t, 0, 0, H)
            store_y(0, t, t + 1, 0, H)
            second_half(1, t)
        for t in range(2, PACK):
            gate(t, 1)
        yb0 = tile([P, PACK * H], BF16, "yb0")
        for c in range(2):
            nc.gpsimd.tensor_scalar(
                yb0[:, c * PACK * C : (c + 1) * PACK * C].rearrange("p (j t) -> p j t", t=PACK),
                y[0][:, :, c * C : (c + 1) * C].rearrange("p t j -> p j t"),
                1.0,
                -0.0,
                MULT,
                ADD,
            )
        yb1 = [tile([P, PACK * C], BF16, "yb1%d" % c) for c in range(2)]
        for t in range(PACK):
            let_through(t, 1, 0, C)
        store_y(1, 0, PACK, 0, C)
        weave(nc.scalar.copy, yb1[0][:], y[1][:, :, 0:C])
        for t in range(PACK):
            let_through(t, 1, C, H)
            if t % 2 == 1:
                store_y(1, t - 1, t + 1, C, H)
        quantise_y(yb0[:], 0, H)
        weave(nc.vector.tensor_copy, yb1[1][:], y[1][:, :, C:H])
        quantise_y(yb1[0][:], H, H + C)
        quantise_y(yb1[1][:], H + C, J)
        for q in range(4):
            queue = nc.scalar if q % 2 else nc.sync
            queue.dma_start(out=out_2[0, 4 * q : 4 * q + 4, :].bitcast(I32), in_=y_scales[32 * q : 32 * q + 4, :].bitcast(I32))
